import numpy as np
import ml_dtypes


def mxq(x, axis, fmt="e4m3"):
    dtype, down = {"e4m3": (ml_dtypes.float8_e4m3fn, 7), "e5m2": (ml_dtypes.float8_e5m2, 14)}[fmt]
    v = np.moveaxis(np.asarray(x, np.float32).astype(ml_dtypes.bfloat16).astype(np.float64), axis, -1)
    blocks = v.reshape(v.shape[:-1] + (-1, 32))
    amax = np.abs(blocks).max(-1, keepdims=True)
    byte = np.maximum(np.where(amax > 0, np.frexp(amax)[1] - 1 + 127, 0) - down, 1)
    scale = np.exp2(byte - 127.0)
    codes = (blocks / scale).astype(np.float32).astype(dtype).astype(np.float64)
    return np.moveaxis((codes * scale).reshape(v.shape), -1, axis)


WIDE = False


def mx_kscale(k):
    if not WIDE:
        return np.ones(k)
    levels = np.array([10, -10, 5, -5, 0])
    if k % 512:
        return np.exp2(np.random.permutation(np.resize(levels, k // 32))).repeat(32)
    a = np.empty((k // 512, 16))
    for p in range(k // 512):
        a[p, :8] = np.random.permutation(np.resize(levels, 8))
        for g in range(8):
            far = levels[np.abs(levels - a[p, g]) >= 10]
            a[p, g + 8] = far[np.random.randint(len(far))]
    return np.exp2(a.ravel()).repeat(32)


def f64(x):
    return np.asarray(x).astype(np.float64)


def striped(idx):
    return np.tile(np.asarray(idx).reshape(-1, 16).T, (8, 1)).astype(np.uint16)


def unstriped(offs):
    return offs[:16].T.reshape(-1).astype(np.int64)


E2M1 = np.array([0.0, 0.5, 1.0, 1.5, 2.0, 3.0, 4.0, 6.0, -0.0, -0.5, -1.0, -1.5, -2.0, -3.0, -4.0, -6.0])


def pack_weight(w, fmt):
    k, n = w.shape
    w = f64(np.asarray(w, np.float32).astype(ml_dtypes.bfloat16)).reshape(k // 32, 32, n)
    amax = np.abs(w).max(1)
    if fmt == "e4m3":
        byte = np.frexp(amax)[1] - 1 + 127 - 7
    else:
        mant, ex = np.frexp(amax / 6.0)
        byte = np.where(mant > 0.5, ex, ex - 1) + 127
    byte = np.clip(np.where(amax > 0, byte, 1), 1, 254)
    scaled = (w * np.exp2(127.0 - byte)[:, None, :]).reshape(k, n).astype(np.float32)
    by_word = np.ascontiguousarray(scaled.reshape(k // 512, 128, 4, n).transpose(0, 1, 3, 2))
    if fmt == "e4m3":
        words = by_word.astype(ml_dtypes.float8_e4m3fn).view(np.uint8)
    else:
        c = by_word.astype(ml_dtypes.float4_e2m1fn).view(np.uint8) & 0xF
        words = (c[..., 0::2] | (c[..., 1::2] << 4)).reshape(k // 512, 128, 2 * n)
    return np.ascontiguousarray(words), np.ascontiguousarray(byte.astype(np.uint8).reshape(k // 512, 16, n))


def unpack_weight(words, scales, fmt):
    g, _, n = scales.shape
    words = np.ascontiguousarray(words).reshape(g, 128, n, -1)
    if fmt == "e4m3":
        vals = words.view(ml_dtypes.float8_e4m3fn).astype(np.float64)
    else:
        nib = np.empty((g, 128, n, 4), np.uint8)
        nib[..., 0::2] = words & 0xF
        nib[..., 1::2] = words >> 4
        vals = E2M1[nib]
    vals = vals * np.repeat(np.exp2(scales.astype(np.float64) - 127.0), 8, axis=1)[..., None]
    return vals.transpose(0, 1, 3, 2).reshape(g * 512, n)


K, T, J, B, R, V, N, Z = 1024, 1024, 384, 48, 512, 512, 256, 512


def setup_inputs():
    n = np.random.standard_normal
    idx = np.random.permutation(T)[:J]
    idx2 = np.random.permutation(V)[:J]
    idx3 = np.random.permutation(Z)[:J]
    fk = mx_kscale(K)
    fr = mx_kscale(R)
    wp = pack_weight(n((K, R)) * 1 / np.sqrt(K) * fk[:, None] * fr, "e2m1")
    wbp = pack_weight(n((R, N)) * 1 / np.sqrt(R) / fr[:, None], "e2m1")
    return {
        "xf": (n((K, T))).astype(np.float32),
        "fk": (np.random.uniform(0.5, 2.0, (K, 1)) / fk[:, None]).astype(np.float32),
        "w_words": wp[0],
        "w_scales": wp[1],
        "tb": (n((R, V)) * 0.7).astype(np.float32),
        "wb_words": wbp[0],
        "wb_scales": wbp[1],
        "tz": (n((N, Z))).astype(np.float32),
        "offs": striped(idx),
        "offs2": striped(idx2),
        "offs3": striped(idx3),
    }


def reference(xf, fk, w_words, w_scales, tb, wb_words, wb_scales, tz, offs, offs2, offs3):
    idx = unstriped(offs)
    idx2 = unstriped(offs2)
    idx3 = unstriped(offs3)
    wu = unpack_weight(w_words, w_scales, "e2m1")
    wbu = unpack_weight(wb_words, wb_scales, "e2m1")
    xg = f64(xf)[:, idx]
    g1 = xg.reshape(K, B, J // B).mean(axis=2)
    g2 = np.repeat(g1, J // B, axis=1)
    u = (xg - g2) * f64(fk)
    uq = mxq(u, 0, "e4m3")
    a = wu.T @ uq
    hid = np.maximum(a, 0.0) * f64(tb)[:, idx2]
    hidq = mxq(hid, 0, "e4m3")
    p = wbu.T @ hidq
    y = p * f64(tz)[:, idx3]
    return y

@@ -1,0 +1,170 @@
+from contextlib import ExitStack
+
+import concourse.mybir as mybir
+
+K, T, J, R, V, N, Z = 1024, 1024, 384, 512, 512, 256, 512
+GROUP = 8
+P = 128
+PACK = 4
+PASSES = K // (P * PACK)
+CHUNK = 128
+CHUNKS = J // CHUNK
+HALVES = N // P
+
+FLOPS = 2 * K * R * J + 2 * R * N * J
+
+F32 = mybir.dt.float32
+BF16 = mybir.dt.bfloat16
+I32 = mybir.dt.int32
+U32 = mybir.dt.uint32
+U16 = mybir.dt.uint16
+U8 = mybir.dt.uint8
+FP8X4 = mybir.dt.float8_e4m3fn_x4
+FP4X4 = mybir.dt.float4_e2m1fn_x4
+ALU = mybir.AluOpType
+COPY = mybir.ActivationFunctionType.Copy
+AXIS_X = mybir.AxisListType.X
+
+
+def tile_list_centredpicks_timestable_timeslook_kernel(
+    tc, xf, fk, w_words, w_scales, tb, wb_words, wb_scales, tz, offs, offs2, offs3, out
+):
+    nc = tc.nc
+    with ExitStack() as ctx:
+        keep = ctx.enter_context(tc.tile_pool(name="keep", bufs=1))
+        psum = ctx.enter_context(tc.psum_pool(name="psum", bufs=1))
+
+        list_x = keep.tile([P, J // 16], U16, name="list_x")
+        list_b = keep.tile([P, J // 16], U16, name="list_b")
+        list_z = keep.tile([P, J // 16], U16, name="list_z")
+        w_raw = keep.tile([P, PASSES, 2 * R], U8, name="w_raw", align_bytes=64)
+        ws_raw = keep.tile([P, PASSES, R], U8, name="ws_raw", align_bytes=64)
+        w_dealt = keep.tile([P, PASSES, 2 * R], U8, name="w_dealt", align_bytes=64)
+        ws_dealt = keep.tile([P, PASSES, R], U8, name="ws_dealt", align_bytes=64)
+        wb_sb = keep.tile([P, 2 * N], U8, name="wb_sb", align_bytes=64)
+        wbs_sb = keep.tile([P, N], U8, name="wbs_sb", align_bytes=64)
+        fk_sb = keep.tile([P, PASSES, 8], F32, name="fk_sb")
+        x_rows = [keep.tile([P, T], F32, name="x_rows%d" % i) for i in range(PASSES * PACK)]
+        tb_rows = [keep.tile([P, V], F32, name="tb_rows%d" % t) for t in range(PACK)]
+        tz_rows = [keep.tile([P, Z], F32, name="tz_rows%d" % h) for h in range(HALVES)]
+
+        nc.vector.memset(ws_raw[:].bitcast(I32), 0)
+        nc.gpsimd.memset(wbs_sb[:].bitcast(I32), 0)
+
+        xf_planes = xf.rearrange("(a p t) c -> a t p c", a=PASSES, t=PACK)
+        tb_planes = tb.rearrange("(p t) c -> t p c", t=PACK)
+
+        nc.sync.dma_start(list_x[:], offs)
+        nc.sync.dma_start(w_raw[:].bitcast(I32), w_words.rearrange("a p c -> p a c").bitcast(I32))
+        nc.sync.dma_start(x_rows[0][:], xf_planes[0, 0])
+        for q in range(4):
+            nc.scalar.dma_start(
+                ws_raw[32 * q : 32 * q + 4, :, :].bitcast(I32),
+                w_scales[:, 4 * q : 4 * q + 4, :].rearrange("a r c -> r a c").bitcast(I32),
+            )
+        nc.sync.dma_start(fk_sb[:, :, 0:PACK], fk.rearrange("(a p t) o -> p a (t o)", a=PASSES, t=PACK))
+        for i in range(1, PASSES * PACK):
+            nc.sync.dma_start(x_rows[i][:], xf_planes[i // PACK, i % PACK])
+        nc.sync.dma_start(list_b[:], offs2)
+        for t in range(PACK):
+            nc.sync.dma_start(tb_rows[t][:], tb_planes[t])
+        nc.sync.dma_start(list_z[:], offs3)
+        nc.sync.dma_start(wb_sb[:].bitcast(I32), wb_words[0].bitcast(I32))
+        for h in range(HALVES):
+            nc.sync.dma_start(tz_rows[h][:], tz[h * P : (h + 1) * P, :])
+        for q in range(4):
+            nc.gpsimd.dma_start(
+                wbs_sb[32 * q : 32 * q + 4, :].bitcast(I32),
+                wb_scales[0, 4 * q : 4 * q + 4, :].bitcast(I32),
+            )
+
+        nc.vector.tensor_copy(
+            w_dealt[:].bitcast(U16).rearrange("p a (t m) -> p a t m", t=PACK),
+            w_raw[:].bitcast(U16).rearrange("p a (m t) -> p a t m", t=PACK),
+        )
+        nc.vector.tensor_copy(
+            ws_dealt[:].rearrange("p a (t m) -> p a t m", t=PACK),
+            ws_raw[:].rearrange("p a (m t) -> p a t m", t=PACK),
+        )
+
+        banks_a = [psum.tile([P, PACK, CHUNK], F32, name="bank_a%d" % c) for c in range(CHUNKS)]
+        banks_p = [psum.tile([P, HALVES, CHUNK], F32, name="bank_p%d" % c) for c in range(CHUNKS)]
+
+        for a in range(PASSES):
+            u_planes = keep.tile([P, PACK, J], BF16, name="u_planes%d" % a)
+            for t in range(PACK):
+                i = a * PACK + t
+                picked = keep.tile([P, J], F32, name="picked%d" % i)
+                sums = keep.tile([P, J // GROUP], F32, name="sums%d" % i)
+                means = keep.tile([P, J // GROUP], F32, name="means%d" % i)
+                nc.scalar.activation(picked[:], x_rows[i][:].indirect(list_x[:]), COPY)
+                by_group = picked[:].rearrange("p (b s) -> p b s", s=GROUP)
+                nc.vector.tensor_reduce(sums[:], by_group, AXIS_X, ALU.add)
+                nc.vector.tensor_scalar(means[:], sums[:], fk_sb[:, a, t : t + 1], 1.0 / GROUP, ALU.mult, ALU.mult)
+                nc.vector.scalar_tensor_tensor(
+                    u_planes[:, t, :].rearrange("p (b s) -> p b s", s=GROUP),
+                    by_group,
+                    fk_sb[:, a, t : t + 1],
+                    means[:].unsqueeze(2).to_broadcast([P, J // GROUP, GROUP]),
+                    ALU.mult,
+                    ALU.subtract,
+                )
+            widths = [J] if a < PASSES - 1 else [CHUNK] * CHUNKS
+            j0 = 0
+            for width in widths:
+                woven = keep.tile([P, width, PACK], BF16, name="u_woven%d_%d" % (a, j0), align_bytes=64)
+                codes = keep.tile([P, width], U32, name="u_codes%d_%d" % (a, j0), align_bytes=64)
+                scales = keep.tile([P, width], U8, name="u_scales%d_%d" % (a, j0), align_bytes=64)
+                nc.vector.tensor_copy(
+                    woven[:].rearrange("p (c i) t -> p c t i", i=4),
+                    u_planes[:, :, j0 : j0 + width].rearrange("p t (c i) -> p c t i", i=4),
+                )
+                nc.vector.quantize_mx(codes[:].bitcast(FP8X4), scales[:], woven[:].rearrange("p j t -> p (j t)"))
+                for c0 in range(0, width, CHUNK):
+                    for t in range(PACK):
+                        nc.tensor.matmul_mx(
+                            banks_a[(j0 + c0) // CHUNK][:, t, :],
+                            lhsT=w_dealt[:, a, 2 * P * t : 2 * P * (t + 1)].bitcast(FP4X4),
+                            lhsT_scale=ws_dealt[:, a, P * t : P * (t + 1)],
+                            rhs=codes[:, c0 : c0 + CHUNK].bitcast(FP8X4),
+                            rhs_scale=scales[:, c0 : c0 + CHUNK],
+                            start=(a == 0 and t == 0),
+                            stop=(a == PASSES - 1 and t == PACK - 1),
+                        )
+                j0 += width
+
+        tb_picked = keep.tile([P, PACK, J], F32, name="tb_picked")
+        for t in range(PACK):
+            nc.scalar.activation(tb_picked[:, t, :], tb_rows[t][:].indirect(list_b[:]), COPY)
+        tz_picked = keep.tile([P, HALVES, J], F32, name="tz_picked")
+        for h in range(HALVES):
+            nc.scalar.activation(tz_picked[:, h, :], tz_rows[h][:].indirect(list_z[:]), COPY)
+
+        out_rows = out.rearrange("(h p) j -> p h j", p=P)
+        for c in range(CHUNKS):
+            cols = slice(c * CHUNK, (c + 1) * CHUNK)
+            hid = keep.tile([P, CHUNK, PACK], BF16, name="hid%d" % c, align_bytes=64)
+            codes = keep.tile([P, CHUNK], U32, name="hid_codes%d" % c, align_bytes=64)
+            scales = keep.tile([P, CHUNK], U8, name="hid_scales%d" % c, align_bytes=64)
+            nc.vector.scalar_tensor_tensor(
+                hid[:],
+                banks_a[c][:].rearrange("p t j -> p j t"),
+                0.0,
+                tb_picked[:, :, cols].rearrange("p t j -> p j t"),
+                ALU.max,
+                ALU.mult,
+            )
+            nc.vector.quantize_mx(codes[:].bitcast(FP8X4), scales[:], hid[:].rearrange("p j t -> p (j t)"))
+            for h in range(HALVES):
+                nc.tensor.matmul_mx(
+                    banks_p[c][:, h, :],
+                    lhsT=wb_sb[:, 2 * P * h : 2 * P * (h + 1)].bitcast(FP4X4),
+                    lhsT_scale=wbs_sb[:, P * h : P * (h + 1)],
+                    rhs=codes[:].bitcast(FP8X4),
+                    rhs_scale=scales[:],
+                    start=True,
+                    stop=True,
+                )
+            result = keep.tile([P, HALVES, CHUNK], F32, name="result%d" % c)
+            nc.vector.tensor_tensor(result[:], banks_p[c][:], tz_picked[:, :, cols], ALU.mult)
+            nc.sync.dma_start(out_rows[:, :, cols], result[:])

@@ -39,8 +39,6 @@ def tile_list_centredpicks_timestable_timeslook_kernel(
         list_z = keep.tile([P, J // 16], U16, name="list_z")
         w_raw = keep.tile([P, PASSES, 2 * R], U8, name="w_raw", align_bytes=64)
         ws_raw = keep.tile([P, PASSES, R], U8, name="ws_raw", align_bytes=64)
-        w_dealt = keep.tile([P, PASSES, 2 * R], U8, name="w_dealt", align_bytes=64)
-        ws_dealt = keep.tile([P, PASSES, R], U8, name="ws_dealt", align_bytes=64)
         wb_sb = keep.tile([P, 2 * N], U8, name="wb_sb", align_bytes=64)
         wbs_sb = keep.tile([P, N], U8, name="wbs_sb", align_bytes=64)
         fk_sb = keep.tile([P, PASSES, 8], F32, name="fk_sb")
@@ -48,113 +46,152 @@ def tile_list_centredpicks_timestable_timeslook_kernel(
         tb_rows = [keep.tile([P, V], F32, name="tb_rows%d" % t) for t in range(PACK)]
         tz_rows = [keep.tile([P, Z], F32, name="tz_rows%d" % h) for h in range(HALVES)]
 
-        nc.vector.memset(ws_raw[:].bitcast(I32), 0)
+        nc.gpsimd.memset(ws_raw[:].bitcast(I32), 0)
         nc.gpsimd.memset(wbs_sb[:].bitcast(I32), 0)
 
         xf_planes = xf.rearrange("(a p t) c -> a t p c", a=PASSES, t=PACK)
         tb_planes = tb.rearrange("(p t) c -> t p c", t=PACK)
 
+        def load_x(i):
+            nc.sync.dma_start(x_rows[i][:], xf_planes[i // PACK, i % PACK])
+
+        nc.sync.dma_start(fk_sb[:, :, 0:PACK], fk.rearrange("(a p t) o -> p a (t o)", a=PASSES, t=PACK))
+        load_x(0)
         nc.sync.dma_start(list_x[:], offs)
-        nc.sync.dma_start(w_raw[:].bitcast(I32), w_words.rearrange("a p c -> p a c").bitcast(I32))
-        nc.sync.dma_start(x_rows[0][:], xf_planes[0, 0])
+        load_x(1)
         for q in range(4):
-            nc.scalar.dma_start(
+            nc.sync.dma_start(
                 ws_raw[32 * q : 32 * q + 4, :, :].bitcast(I32),
                 w_scales[:, 4 * q : 4 * q + 4, :].rearrange("a r c -> r a c").bitcast(I32),
             )
-        nc.sync.dma_start(fk_sb[:, :, 0:PACK], fk.rearrange("(a p t) o -> p a (t o)", a=PASSES, t=PACK))
-        for i in range(1, PASSES * PACK):
-            nc.sync.dma_start(x_rows[i][:], xf_planes[i // PACK, i % PACK])
+        nc.sync.dma_start(w_raw[:].bitcast(I32), w_words.rearrange("a p c -> p a c").bitcast(I32))
+        load_x(2)
+        load_x(3)
         nc.sync.dma_start(list_b[:], offs2)
+        nc.sync.dma_start(list_z[:], offs3)
+        for i in range(PACK, PASSES * PACK):
+            load_x(i)
         for t in range(PACK):
             nc.sync.dma_start(tb_rows[t][:], tb_planes[t])
-        nc.sync.dma_start(list_z[:], offs3)
-        nc.sync.dma_start(wb_sb[:].bitcast(I32), wb_words[0].bitcast(I32))
-        for h in range(HALVES):
-            nc.sync.dma_start(tz_rows[h][:], tz[h * P : (h + 1) * P, :])
         for q in range(4):
-            nc.gpsimd.dma_start(
+            nc.sync.dma_start(
                 wbs_sb[32 * q : 32 * q + 4, :].bitcast(I32),
                 wb_scales[0, 4 * q : 4 * q + 4, :].bitcast(I32),
             )
+        nc.sync.dma_start(wb_sb[:].bitcast(I32), wb_words[0].bitcast(I32))
+        for h in range(HALVES):
+            nc.sync.dma_start(tz_rows[h][:], tz[h * P : (h + 1) * P, :])
 
+        banks_a = [psum.tile([P, PACK, CHUNK], F32, name="bank_a%d" % c) for c in range(CHUNKS)]
+        banks_p = [psum.tile([P, HALVES, CHUNK], F32, name="bank_p%d" % c) for c in range(CHUNKS)]
+        chunks = [slice(c * CHUNK, (c + 1) * CHUNK) for c in range(CHUNKS)]
+        whole = [slice(0, J)]
+
+        def gather(dst, rows, offsets, cols):
+            nc.scalar.activation(dst[:, cols], rows[:].indirect(offsets[:, cols.start // 16 : cols.stop // 16]), COPY)
+
+        groups = J // GROUP
+        fk_eighth = keep.tile([P, PASSES, PACK], F32, name="fk_eighth")
+        chunk_groups = CHUNK // GROUP
+        scaled = [keep.tile([P, PACK, J], F32, name="scaled%d" % a) for a in range(PASSES)]
+        sums = [keep.tile([P, PACK, groups], F32, name="sums%d" % a) for a in range(PASSES)]
+        means = [keep.tile([P, groups, PACK], F32, name="means%d" % a) for a in range(PASSES)]
+        u_woven = [
+            [keep.tile([P, CHUNK, PACK], BF16, name="u_woven%d_%d" % (a, c), align_bytes=64) for c in range(CHUNKS)]
+            for a in range(PASSES)
+        ]
+
+        def pick(i):
+            a, t = divmod(i, PACK)
+            picked = keep.tile([P, J], F32, name="picked%d" % i, tag="picked%d" % i, align_bytes=64)
+            gather(picked, x_rows[i], list_x, whole[0])
+            nc.gpsimd.tensor_scalar(scaled[a][:, t, :], picked[:], fk_sb[:, a, t : t + 1], 0.0, ALU.mult, ALU.add)
+            nc.vector.tensor_reduce(
+                sums[a][:, t, :], picked[:].rearrange("p (b s) -> p b s", s=GROUP), AXIS_X, ALU.add
+            )
+
+        def group_means(a):
+            nc.vector.tensor_tensor(
+                means[a][:],
+                sums[a][:].rearrange("p t b -> p b t"),
+                fk_eighth[:, a, :].unsqueeze(1).to_broadcast([P, groups, PACK]),
+                ALU.mult,
+            )
+
+        def centre(a, c):
+            nc.vector.tensor_tensor(
+                u_woven[a][c][:].rearrange("p (b s) t -> p b t s", s=GROUP),
+                scaled[a][:, :, chunks[c]].rearrange("p t (b s) -> p b t s", s=GROUP),
+                means[a][:, c * chunk_groups : (c + 1) * chunk_groups, :]
+                .unsqueeze(3)
+                .to_broadcast([P, chunk_groups, PACK, GROUP]),
+                ALU.subtract,
+            )
+
+        def first_product(a, c, w_dealt, ws_dealt):
+            codes = keep.tile([P, CHUNK], U32, name="u_codes%d_%d" % (a, c), align_bytes=64)
+            scales = keep.tile([P, CHUNK], U8, name="u_scales%d_%d" % (a, c), align_bytes=64)
+            nc.vector.quantize_mx(codes[:].bitcast(FP8X4), scales[:], u_woven[a][c][:].rearrange("p j t -> p (j t)"))
+            for t in range(PACK):
+                nc.tensor.matmul_mx(
+                    banks_a[c][:, t, :],
+                    lhsT=w_dealt[:, a, 2 * P * t : 2 * P * (t + 1)].bitcast(FP4X4),
+                    lhsT_scale=ws_dealt[:, a, P * t : P * (t + 1)],
+                    rhs=codes[:].bitcast(FP8X4),
+                    rhs_scale=scales[:],
+                    start=(a == 0 and t == 0),
+                    stop=(a == PASSES - 1 and t == PACK - 1),
+                )
+
+        nc.scalar.activation(fk_eighth[:], fk_sb[:, :, 0:PACK], COPY, scale=1.0 / GROUP)
+        pick(0)
+        w_dealt = keep.tile([P, PASSES, 2 * R], U8, name="w_dealt", tag="picked0", align_bytes=64)
         nc.vector.tensor_copy(
             w_dealt[:].bitcast(U16).rearrange("p a (t m) -> p a t m", t=PACK),
             w_raw[:].bitcast(U16).rearrange("p a (m t) -> p a t m", t=PACK),
         )
+        pick(1)
+        ws_dealt = keep.tile([P, PASSES, R], U8, name="ws_dealt", tag="picked1", align_bytes=64)
         nc.vector.tensor_copy(
             ws_dealt[:].rearrange("p a (t m) -> p a t m", t=PACK),
             ws_raw[:].rearrange("p a (m t) -> p a t m", t=PACK),
         )
-
-        banks_a = [psum.tile([P, PACK, CHUNK], F32, name="bank_a%d" % c) for c in range(CHUNKS)]
-        banks_p = [psum.tile([P, HALVES, CHUNK], F32, name="bank_p%d" % c) for c in range(CHUNKS)]
-
         for a in range(PASSES):
-            u_planes = keep.tile([P, PACK, J], BF16, name="u_planes%d" % a)
-            for t in range(PACK):
-                i = a * PACK + t
-                picked = keep.tile([P, J], F32, name="picked%d" % i)
-                sums = keep.tile([P, J // GROUP], F32, name="sums%d" % i)
-                means = keep.tile([P, J // GROUP], F32, name="means%d" % i)
-                nc.scalar.activation(picked[:], x_rows[i][:].indirect(list_x[:]), COPY)
-                by_group = picked[:].rearrange("p (b s) -> p b s", s=GROUP)
-                nc.vector.tensor_reduce(sums[:], by_group, AXIS_X, ALU.add)
-                nc.vector.tensor_scalar(means[:], sums[:], fk_sb[:, a, t : t + 1], 1.0 / GROUP, ALU.mult, ALU.mult)
-                nc.vector.scalar_tensor_tensor(
-                    u_planes[:, t, :].rearrange("p (b s) -> p b s", s=GROUP),
-                    by_group,
-                    fk_sb[:, a, t : t + 1],
-                    means[:].unsqueeze(2).to_broadcast([P, J // GROUP, GROUP]),
-                    ALU.mult,
-                    ALU.subtract,
-                )
-            widths = [J] if a < PASSES - 1 else [CHUNK] * CHUNKS
-            j0 = 0
-            for width in widths:
-                woven = keep.tile([P, width, PACK], BF16, name="u_woven%d_%d" % (a, j0), align_bytes=64)
-                codes = keep.tile([P, width], U32, name="u_codes%d_%d" % (a, j0), align_bytes=64)
-                scales = keep.tile([P, width], U8, name="u_scales%d_%d" % (a, j0), align_bytes=64)
-                nc.vector.tensor_copy(
-                    woven[:].rearrange("p (c i) t -> p c t i", i=4),
-                    u_planes[:, :, j0 : j0 + width].rearrange("p t (c i) -> p c t i", i=4),
-                )
-                nc.vector.quantize_mx(codes[:].bitcast(FP8X4), scales[:], woven[:].rearrange("p j t -> p (j t)"))
-                for c0 in range(0, width, CHUNK):
-                    for t in range(PACK):
-                        nc.tensor.matmul_mx(
-                            banks_a[(j0 + c0) // CHUNK][:, t, :],
-                            lhsT=w_dealt[:, a, 2 * P * t : 2 * P * (t + 1)].bitcast(FP4X4),
-                            lhsT_scale=ws_dealt[:, a, P * t : P * (t + 1)],
-                            rhs=codes[:, c0 : c0 + CHUNK].bitcast(FP8X4),
-                            rhs_scale=scales[:, c0 : c0 + CHUNK],
-                            start=(a == 0 and t == 0),
-                            stop=(a == PASSES - 1 and t == PACK - 1),
-                        )
-                j0 += width
+            for i in range(max(a * PACK, 2), (a + 1) * PACK):
+                pick(i)
+            group_means(a)
+            centre(a, 0)
+            centre(a, 1)
+            first_product(a, 0, w_dealt, ws_dealt)
+            centre(a, 2)
+            first_product(a, 1, w_dealt, ws_dealt)
+            first_product(a, 2, w_dealt, ws_dealt)
 
         tb_picked = keep.tile([P, PACK, J], F32, name="tb_picked")
         for t in range(PACK):
-            nc.scalar.activation(tb_picked[:, t, :], tb_rows[t][:].indirect(list_b[:]), COPY)
+            for cols in chunks if t == PACK - 1 else whole:
+                gather(tb_picked[:, t, :], tb_rows[t], list_b, cols)
         tz_picked = keep.tile([P, HALVES, J], F32, name="tz_picked")
         for h in range(HALVES):
-            nc.scalar.activation(tz_picked[:, h, :], tz_rows[h][:].indirect(list_z[:]), COPY)
+            for cols in chunks if h == HALVES - 1 else whole:
+                gather(tz_picked[:, h, :], tz_rows[h], list_z, cols)
 
-        out_rows = out.rearrange("(h p) j -> p h j", p=P)
-        for c in range(CHUNKS):
-            cols = slice(c * CHUNK, (c + 1) * CHUNK)
-            hid = keep.tile([P, CHUNK, PACK], BF16, name="hid%d" % c, align_bytes=64)
-            codes = keep.tile([P, CHUNK], U32, name="hid_codes%d" % c, align_bytes=64)
-            scales = keep.tile([P, CHUNK], U8, name="hid_scales%d" % c, align_bytes=64)
+        hid = [keep.tile([P, CHUNK, PACK], BF16, name="hid%d" % c, align_bytes=64) for c in range(CHUNKS)]
+
+        def hidden(c):
             nc.vector.scalar_tensor_tensor(
-                hid[:],
+                hid[c][:],
                 banks_a[c][:].rearrange("p t j -> p j t"),
                 0.0,
-                tb_picked[:, :, cols].rearrange("p t j -> p j t"),
+                tb_picked[:, :, chunks[c]].rearrange("p t j -> p j t"),
                 ALU.max,
                 ALU.mult,
             )
-            nc.vector.quantize_mx(codes[:].bitcast(FP8X4), scales[:], hid[:].rearrange("p j t -> p (j t)"))
+
+        def second_product(c):
+            codes = keep.tile([P, CHUNK], U32, name="hid_codes%d" % c, align_bytes=64)
+            scales = keep.tile([P, CHUNK], U8, name="hid_scales%d" % c, align_bytes=64)
+            nc.vector.quantize_mx(codes[:].bitcast(FP8X4), scales[:], hid[c][:].rearrange("p j t -> p (j t)"))
             for h in range(HALVES):
                 nc.tensor.matmul_mx(
                     banks_p[c][:, h, :],
@@ -165,6 +202,19 @@ def tile_list_centredpicks_timestable_timeslook_kernel(
                     start=True,
                     stop=True,
                 )
+
+        out_rows = out.rearrange("(h p) j -> p h j", p=P)
+
+        def finish(c):
             result = keep.tile([P, HALVES, CHUNK], F32, name="result%d" % c)
-            nc.vector.tensor_tensor(result[:], banks_p[c][:], tz_picked[:, :, cols], ALU.mult)
-            nc.sync.dma_start(out_rows[:, :, cols], result[:])
+            nc.vector.tensor_tensor(result[:], banks_p[c][:], tz_picked[:, :, chunks[c]], ALU.mult)
+            nc.sync.dma_start(out_rows[:, :, chunks[c]], result[:])
+
+        hidden(0)
+        hidden(1)
+        second_product(0)
+        hidden(2)
+        second_product(1)
+        second_product(2)
+        for c in range(CHUNKS):
+            finish(c)

@@ -64,15 +64,15 @@ def tile_list_centredpicks_timestable_timeslook_kernel(
                 ws_raw[32 * q : 32 * q + 4, :, :].bitcast(I32),
                 w_scales[:, 4 * q : 4 * q + 4, :].rearrange("a r c -> r a c").bitcast(I32),
             )
-        nc.sync.dma_start(w_raw[:].bitcast(I32), w_words.rearrange("a p c -> p a c").bitcast(I32))
         load_x(2)
         load_x(3)
-        nc.sync.dma_start(list_b[:], offs2)
-        nc.sync.dma_start(list_z[:], offs3)
+        nc.sync.dma_start(w_raw[:].bitcast(I32), w_words.rearrange("a p c -> p a c").bitcast(I32))
         for i in range(PACK, PASSES * PACK):
             load_x(i)
+        nc.sync.dma_start(list_b[:], offs2)
         for t in range(PACK):
             nc.sync.dma_start(tb_rows[t][:], tb_planes[t])
+        nc.sync.dma_start(list_z[:], offs3)
         for q in range(4):
             nc.sync.dma_start(
                 wbs_sb[32 * q : 32 * q + 4, :].bitcast(I32),
@@ -92,80 +92,97 @@ def tile_list_centredpicks_timestable_timeslook_kernel(
 
         groups = J // GROUP
         fk_eighth = keep.tile([P, PASSES, PACK], F32, name="fk_eighth")
-        chunk_groups = CHUNK // GROUP
         scaled = [keep.tile([P, PACK, J], F32, name="scaled%d" % a) for a in range(PASSES)]
         sums = [keep.tile([P, PACK, groups], F32, name="sums%d" % a) for a in range(PASSES)]
         means = [keep.tile([P, groups, PACK], F32, name="means%d" % a) for a in range(PASSES)]
-        u_woven = [
-            [keep.tile([P, CHUNK, PACK], BF16, name="u_woven%d_%d" % (a, c), align_bytes=64) for c in range(CHUNKS)]
-            for a in range(PASSES)
-        ]
+        woven = [keep.tile([P, J, PACK], BF16, name="woven%d" % a, align_bytes=64) for a in range(PASSES)]
+        first_and_rest = [chunks[0], slice(CHUNK, J)]
 
-        def pick(i):
+        def groups_of(cols):
+            return slice(cols.start // GROUP, cols.stop // GROUP)
+
+        def pick(i, pieces):
             a, t = divmod(i, PACK)
             picked = keep.tile([P, J], F32, name="picked%d" % i, tag="picked%d" % i, align_bytes=64)
-            gather(picked, x_rows[i], list_x, whole[0])
-            nc.gpsimd.tensor_scalar(scaled[a][:, t, :], picked[:], fk_sb[:, a, t : t + 1], 0.0, ALU.mult, ALU.add)
-            nc.vector.tensor_reduce(
-                sums[a][:, t, :], picked[:].rearrange("p (b s) -> p b s", s=GROUP), AXIS_X, ALU.add
-            )
+            for cols in pieces:
+                gather(picked, x_rows[i], list_x, cols)
+                nc.gpsimd.tensor_scalar(
+                    scaled[a][:, t, cols], picked[:, cols], fk_sb[:, a, t : t + 1], 0.0, ALU.mult, ALU.add
+                )
+                nc.vector.tensor_reduce(
+                    sums[a][:, t, groups_of(cols)],
+                    picked[:, cols].rearrange("p (b s) -> p b s", s=GROUP),
+                    AXIS_X,
+                    ALU.add,
+                )
 
-        def group_means(a):
+        def group_means(a, cols):
+            some = groups_of(cols)
             nc.vector.tensor_tensor(
-                means[a][:],
-                sums[a][:].rearrange("p t b -> p b t"),
-                fk_eighth[:, a, :].unsqueeze(1).to_broadcast([P, groups, PACK]),
+                means[a][:, some, :],
+                sums[a][:, :, some].rearrange("p t b -> p b t"),
+                fk_eighth[:, a, :].unsqueeze(1).to_broadcast([P, some.stop - some.start, PACK]),
                 ALU.mult,
             )
 
-        def centre(a, c):
+        def centre(a, cols):
+            some = groups_of(cols)
             nc.vector.tensor_tensor(
-                u_woven[a][c][:].rearrange("p (b s) t -> p b t s", s=GROUP),
-                scaled[a][:, :, chunks[c]].rearrange("p t (b s) -> p b t s", s=GROUP),
-                means[a][:, c * chunk_groups : (c + 1) * chunk_groups, :]
-                .unsqueeze(3)
-                .to_broadcast([P, chunk_groups, PACK, GROUP]),
+                woven[a][:, cols, :].rearrange("p (b s) t -> p b t s", s=GROUP),
+                scaled[a][:, :, cols].rearrange("p t (b s) -> p b t s", s=GROUP),
+                means[a][:, some, :].unsqueeze(3).to_broadcast([P, some.stop - some.start, PACK, GROUP]),
                 ALU.subtract,
             )
 
-        def first_product(a, c, w_dealt, ws_dealt):
-            codes = keep.tile([P, CHUNK], U32, name="u_codes%d_%d" % (a, c), align_bytes=64)
-            scales = keep.tile([P, CHUNK], U8, name="u_scales%d_%d" % (a, c), align_bytes=64)
-            nc.vector.quantize_mx(codes[:].bitcast(FP8X4), scales[:], u_woven[a][c][:].rearrange("p j t -> p (j t)"))
-            for t in range(PACK):
-                nc.tensor.matmul_mx(
-                    banks_a[c][:, t, :],
-                    lhsT=w_dealt[:, a, 2 * P * t : 2 * P * (t + 1)].bitcast(FP4X4),
-                    lhsT_scale=ws_dealt[:, a, P * t : P * (t + 1)],
-                    rhs=codes[:].bitcast(FP8X4),
-                    rhs_scale=scales[:],
-                    start=(a == 0 and t == 0),
-                    stop=(a == PASSES - 1 and t == PACK - 1),
-                )
+        def first_product(a, cols, w_dealt, ws_dealt):
+            width = cols.stop - cols.start
+            codes = keep.tile([P, width], U32, name="u_codes%d_%d" % (a, cols.start), align_bytes=64)
+            scales = keep.tile([P, width], U8, name="u_scales%d_%d" % (a, cols.start), align_bytes=64)
+            nc.vector.quantize_mx(codes[:].bitcast(FP8X4), scales[:], woven[a][:, cols, :].rearrange("p j t -> p (j t)"))
+            for j0 in range(0, width, CHUNK):
+                for t in range(PACK):
+                    nc.tensor.matmul_mx(
+                        banks_a[(cols.start + j0) // CHUNK][:, t, :],
+                        lhsT=w_dealt[:, a, 2 * P * t : 2 * P * (t + 1)].bitcast(FP4X4),
+                        lhsT_scale=ws_dealt[:, a, P * t : P * (t + 1)],
+                        rhs=codes[:, j0 : j0 + CHUNK].bitcast(FP8X4),
+                        rhs_scale=scales[:, j0 : j0 + CHUNK],
+                        start=(a == 0 and t == 0),
+                        stop=(a == PASSES - 1 and t == PACK - 1),
+                    )
 
         nc.scalar.activation(fk_eighth[:], fk_sb[:, :, 0:PACK], COPY, scale=1.0 / GROUP)
-        pick(0)
-        w_dealt = keep.tile([P, PASSES, 2 * R], U8, name="w_dealt", tag="picked0", align_bytes=64)
-        nc.vector.tensor_copy(
-            w_dealt[:].bitcast(U16).rearrange("p a (t m) -> p a t m", t=PACK),
-            w_raw[:].bitcast(U16).rearrange("p a (m t) -> p a t m", t=PACK),
-        )
-        pick(1)
+        pick(0, whole)
+        pick(1, whole)
         ws_dealt = keep.tile([P, PASSES, R], U8, name="ws_dealt", tag="picked1", align_bytes=64)
         nc.vector.tensor_copy(
             ws_dealt[:].rearrange("p a (t m) -> p a t m", t=PACK),
             ws_raw[:].rearrange("p a (m t) -> p a t m", t=PACK),
         )
+        pick(2, whole)
+        pick(3, whole)
+        w_dealt = keep.tile([P, PASSES, 2 * R], U8, name="w_dealt", align_bytes=64)
         for a in range(PASSES):
-            for i in range(max(a * PACK, 2), (a + 1) * PACK):
-                pick(i)
-            group_means(a)
-            centre(a, 0)
-            centre(a, 1)
-            first_product(a, 0, w_dealt, ws_dealt)
-            centre(a, 2)
-            first_product(a, 1, w_dealt, ws_dealt)
-            first_product(a, 2, w_dealt, ws_dealt)
+            nc.scalar.copy(
+                w_dealt[:, a, :].bitcast(U16).rearrange("p (t m) -> p t m", t=PACK),
+                w_raw[:, a, :].bitcast(U16).rearrange("p (m t) -> p t m", t=PACK),
+            )
+        group_means(0, whole[0])
+        centre(0, whole[0])
+        first_product(0, whole[0], w_dealt, ws_dealt)
+
+        pick(4, whole)
+        pick(5, whole)
+        pick(6, whole)
+        pick(7, first_and_rest)
+        group_means(1, first_and_rest[0])
+        centre(1, chunks[0])
+        group_means(1, first_and_rest[1])
+        first_product(1, chunks[0], w_dealt, ws_dealt)
+        centre(1, chunks[1])
+        centre(1, chunks[2])
+        first_product(1, chunks[1], w_dealt, ws_dealt)
+        first_product(1, chunks[2], w_dealt, ws_dealt)
 
         tb_picked = keep.tile([P, PACK, J], F32, name="tb_picked")
         for t in range(PACK):

from contextlib import ExitStack

import concourse.mybir as mybir

K, T, J, R, V, N, Z = 1024, 1024, 384, 512, 512, 256, 512
GROUP = 8
P = 128
PACK = 4
PASSES = K // (P * PACK)
CHUNK = 128
CHUNKS = J // CHUNK
HALVES = N // P

FLOPS = 2 * K * R * J + 2 * R * N * J

F32 = mybir.dt.float32
BF16 = mybir.dt.bfloat16
I32 = mybir.dt.int32
U32 = mybir.dt.uint32
U16 = mybir.dt.uint16
U8 = mybir.dt.uint8
FP8X4 = mybir.dt.float8_e4m3fn_x4
FP4X4 = mybir.dt.float4_e2m1fn_x4
ALU = mybir.AluOpType
COPY = mybir.ActivationFunctionType.Copy
AXIS_X = mybir.AxisListType.X


def tile_list_centredpicks_timestable_timeslook_kernel(
    tc, xf, fk, w_words, w_scales, tb, wb_words, wb_scales, tz, offs, offs2, offs3, out
):
    nc = tc.nc
    with ExitStack() as ctx:
        keep = ctx.enter_context(tc.tile_pool(name="keep", bufs=1))
        psum = ctx.enter_context(tc.psum_pool(name="psum", bufs=1))

        list_x = keep.tile([P, J // 16], U16, name="list_x")
        list_b = keep.tile([P, J // 16], U16, name="list_b")
        list_z = keep.tile([P, J // 16], U16, name="list_z")
        w_raw = keep.tile([P, PASSES, 2 * R], U8, name="w_raw", align_bytes=64)
        ws_raw = keep.tile([P, PASSES, R], U8, name="ws_raw", align_bytes=64)
        wb_sb = keep.tile([P, 2 * N], U8, name="wb_sb", align_bytes=64)
        wbs_sb = keep.tile([P, N], U8, name="wbs_sb", align_bytes=64)
        fk_sb = keep.tile([P, PASSES, 8], F32, name="fk_sb")
        x_rows = [keep.tile([P, T], F32, name="x_rows%d" % i) for i in range(PASSES * PACK)]
        tb_rows = [keep.tile([P, V], F32, name="tb_rows%d" % t) for t in range(PACK)]
        tz_rows = [keep.tile([P, Z], F32, name="tz_rows%d" % h) for h in range(HALVES)]

        nc.gpsimd.memset(ws_raw[:].bitcast(I32), 0)
        nc.gpsimd.memset(wbs_sb[:].bitcast(I32), 0)

        xf_planes = xf.rearrange("(a p t) c -> a t p c", a=PASSES, t=PACK)
        tb_planes = tb.rearrange("(p t) c -> t p c", t=PACK)

        def load_x(i):
            nc.sync.dma_start(x_rows[i][:], xf_planes[i // PACK, i % PACK])

        nc.sync.dma_start(fk_sb[:, :, 0:PACK], fk.rearrange("(a p t) o -> p a (t o)", a=PASSES, t=PACK))
        load_x(0)
        nc.sync.dma_start(list_x[:], offs)
        load_x(1)
        for q in range(4):
            nc.sync.dma_start(
                ws_raw[32 * q : 32 * q + 4, :, :].bitcast(I32),
                w_scales[:, 4 * q : 4 * q + 4, :].rearrange("a r c -> r a c").bitcast(I32),
            )
        load_x(2)
        load_x(3)
        nc.sync.dma_start(w_raw[:].bitcast(I32), w_words.rearrange("a p c -> p a c").bitcast(I32))
        for i in range(PACK, PASSES * PACK):
            load_x(i)
        nc.sync.dma_start(list_b[:], offs2)
        for t in range(PACK):
            nc.sync.dma_start(tb_rows[t][:], tb_planes[t])
        nc.sync.dma_start(list_z[:], offs3)
        for q in range(4):
            nc.sync.dma_start(
                wbs_sb[32 * q : 32 * q + 4, :].bitcast(I32),
                wb_scales[0, 4 * q : 4 * q + 4, :].bitcast(I32),
            )
        nc.sync.dma_start(wb_sb[:].bitcast(I32), wb_words[0].bitcast(I32))
        for h in range(HALVES):
            nc.sync.dma_start(tz_rows[h][:], tz[h * P : (h + 1) * P, :])

        banks_a = [psum.tile([P, PACK, CHUNK], F32, name="bank_a%d" % c) for c in range(CHUNKS)]
        banks_p = [psum.tile([P, HALVES, CHUNK], F32, name="bank_p%d" % c) for c in range(CHUNKS)]
        chunks = [slice(c * CHUNK, (c + 1) * CHUNK) for c in range(CHUNKS)]
        whole = [slice(0, J)]

        def gather(dst, rows, offsets, cols):
            nc.scalar.activation(dst[:, cols], rows[:].indirect(offsets[:, cols.start // 16 : cols.stop // 16]), COPY)

        groups = J // GROUP
        fk_eighth = keep.tile([P, PASSES, PACK], F32, name="fk_eighth")
        scaled = [keep.tile([P, PACK, J], F32, name="scaled%d" % a) for a in range(PASSES)]
        sums = [keep.tile([P, PACK, groups], F32, name="sums%d" % a) for a in range(PASSES)]
        means = [keep.tile([P, groups, PACK], F32, name="means%d" % a) for a in range(PASSES)]
        woven = [keep.tile([P, J, PACK], BF16, name="woven%d" % a, align_bytes=64) for a in range(PASSES)]
        first_and_rest = [chunks[0], slice(CHUNK, J)]

        def groups_of(cols):
            return slice(cols.start // GROUP, cols.stop // GROUP)

        def pick(i, pieces):
            a, t = divmod(i, PACK)
            picked = keep.tile([P, J], F32, name="picked%d" % i, tag="picked%d" % i, align_bytes=64)
            for cols in pieces:
                gather(picked, x_rows[i], list_x, cols)
                nc.gpsimd.tensor_scalar(
                    scaled[a][:, t, cols], picked[:, cols], fk_sb[:, a, t : t + 1], 0.0, ALU.mult, ALU.add
                )
                nc.vector.tensor_reduce(
                    sums[a][:, t, groups_of(cols)],
                    picked[:, cols].rearrange("p (b s) -> p b s", s=GROUP),
                    AXIS_X,
                    ALU.add,
                )

        def group_means(a, cols):
            some = groups_of(cols)
            nc.vector.tensor_tensor(
                means[a][:, some, :],
                sums[a][:, :, some].rearrange("p t b -> p b t"),
                fk_eighth[:, a, :].unsqueeze(1).to_broadcast([P, some.stop - some.start, PACK]),
                ALU.mult,
            )

        def centre(a, cols):
            some = groups_of(cols)
            nc.vector.tensor_tensor(
                woven[a][:, cols, :].rearrange("p (b s) t -> p b t s", s=GROUP),
                scaled[a][:, :, cols].rearrange("p t (b s) -> p b t s", s=GROUP),
                means[a][:, some, :].unsqueeze(3).to_broadcast([P, some.stop - some.start, PACK, GROUP]),
                ALU.subtract,
            )

        def first_product(a, cols, w_dealt, ws_dealt):
            width = cols.stop - cols.start
            codes = keep.tile([P, width], U32, name="u_codes%d_%d" % (a, cols.start), align_bytes=64)
            scales = keep.tile([P, width], U8, name="u_scales%d_%d" % (a, cols.start), align_bytes=64)
            nc.vector.quantize_mx(codes[:].bitcast(FP8X4), scales[:], woven[a][:, cols, :].rearrange("p j t -> p (j t)"))
            for j0 in range(0, width, CHUNK):
                for t in range(PACK):
                    nc.tensor.matmul_mx(
                        banks_a[(cols.start + j0) // CHUNK][:, t, :],
                        lhsT=w_dealt[:, a, 2 * P * t : 2 * P * (t + 1)].bitcast(FP4X4),
                        lhsT_scale=ws_dealt[:, a, P * t : P * (t + 1)],
                        rhs=codes[:, j0 : j0 + CHUNK].bitcast(FP8X4),
                        rhs_scale=scales[:, j0 : j0 + CHUNK],
                        start=(a == 0 and t == 0),
                        stop=(a == PASSES - 1 and t == PACK - 1),
                    )

        nc.scalar.activation(fk_eighth[:], fk_sb[:, :, 0:PACK], COPY, scale=1.0 / GROUP)
        pick(0, whole)
        pick(1, whole)
        ws_dealt = keep.tile([P, PASSES, R], U8, name="ws_dealt", tag="picked1", align_bytes=64)
        nc.vector.tensor_copy(
            ws_dealt[:].rearrange("p a (t m) -> p a t m", t=PACK),
            ws_raw[:].rearrange("p a (m t) -> p a t m", t=PACK),
        )
        pick(2, whole)
        pick(3, whole)
        w_dealt = keep.tile([P, PASSES, 2 * R], U8, name="w_dealt", align_bytes=64)
        for a in range(PASSES):
            nc.scalar.copy(
                w_dealt[:, a, :].bitcast(U16).rearrange("p (t m) -> p t m", t=PACK),
                w_raw[:, a, :].bitcast(U16).rearrange("p (m t) -> p t m", t=PACK),
            )
        group_means(0, whole[0])
        centre(0, whole[0])
        first_product(0, whole[0], w_dealt, ws_dealt)

        pick(4, whole)
        pick(5, whole)
        pick(6, whole)
        pick(7, first_and_rest)
        group_means(1, first_and_rest[0])
        centre(1, chunks[0])
        group_means(1, first_and_rest[1])
        first_product(1, chunks[0], w_dealt, ws_dealt)
        centre(1, chunks[1])
        centre(1, chunks[2])
        first_product(1, chunks[1], w_dealt, ws_dealt)
        first_product(1, chunks[2], w_dealt, ws_dealt)

        tb_picked = keep.tile([P, PACK, J], F32, name="tb_picked")
        for t in range(PACK):
            for cols in chunks if t == PACK - 1 else whole:
                gather(tb_picked[:, t, :], tb_rows[t], list_b, cols)
        tz_picked = keep.tile([P, HALVES, J], F32, name="tz_picked")
        for h in range(HALVES):
            for cols in chunks if h == HALVES - 1 else whole:
                gather(tz_picked[:, h, :], tz_rows[h], list_z, cols)

        hid = [keep.tile([P, CHUNK, PACK], BF16, name="hid%d" % c, align_bytes=64) for c in range(CHUNKS)]

        def hidden(c):
            nc.vector.scalar_tensor_tensor(
                hid[c][:],
                banks_a[c][:].rearrange("p t j -> p j t"),
                0.0,
                tb_picked[:, :, chunks[c]].rearrange("p t j -> p j t"),
                ALU.max,
                ALU.mult,
            )

        def second_product(c):
            codes = keep.tile([P, CHUNK], U32, name="hid_codes%d" % c, align_bytes=64)
            scales = keep.tile([P, CHUNK], U8, name="hid_scales%d" % c, align_bytes=64)
            nc.vector.quantize_mx(codes[:].bitcast(FP8X4), scales[:], hid[c][:].rearrange("p j t -> p (j t)"))
            for h in range(HALVES):
                nc.tensor.matmul_mx(
                    banks_p[c][:, h, :],
                    lhsT=wb_sb[:, 2 * P * h : 2 * P * (h + 1)].bitcast(FP4X4),
                    lhsT_scale=wbs_sb[:, P * h : P * (h + 1)],
                    rhs=codes[:].bitcast(FP8X4),
                    rhs_scale=scales[:],
                    start=True,
                    stop=True,
                )

        out_rows = out.rearrange("(h p) j -> p h j", p=P)

        def finish(c):
            result = keep.tile([P, HALVES, CHUNK], F32, name="result%d" % c)
            nc.vector.tensor_tensor(result[:], banks_p[c][:], tz_picked[:, :, chunks[c]], ALU.mult)
            nc.sync.dma_start(out_rows[:, :, chunks[c]], result[:])

        hidden(0)
        hidden(1)
        second_product(0)
        hidden(2)
        second_product(1)
        second_product(2)
        for c in range(CHUNKS):
            finish(c)
